import numpy as np
import ml_dtypes


def mxq(x, axis, fmt="e4m3"):
    dtype, down = {"e4m3": (ml_dtypes.float8_e4m3fn, 7), "e5m2": (ml_dtypes.float8_e5m2, 14)}[fmt]
    v = np.moveaxis(np.asarray(x, np.float32).astype(ml_dtypes.bfloat16).astype(np.float64), axis, -1)
    blocks = v.reshape(v.shape[:-1] + (-1, 32))
    amax = np.abs(blocks).max(-1, keepdims=True)
    byte = np.maximum(np.where(amax > 0, np.frexp(amax)[1] - 1 + 127, 0) - down, 1)
    scale = np.exp2(byte - 127.0)
    codes = (blocks / scale).astype(np.float32).astype(dtype).astype(np.float64)
    return np.moveaxis((codes * scale).reshape(v.shape), -1, axis)


WIDE = False


def mx_kscale(k):
    if not WIDE:
        return np.ones(k)
    levels = np.array([30, -30])
    if k % 512:
        return np.exp2(np.random.permutation(np.resize(levels, k // 32))).repeat(32)
    a = np.empty((k // 512, 16))
    for p in range(k // 512):
        a[p, :8] = np.random.permutation(np.resize(levels, 8))
        for g in range(8):
            far = levels[np.abs(levels - a[p, g]) >= 10]
            a[p, g + 8] = far[np.random.randint(len(far))]
    return np.exp2(a.ravel()).repeat(32)


def f64(x):
    return np.asarray(x).astype(np.float64)


def striped(idx):
    return np.tile(np.asarray(idx).reshape(-1, 16).T, (8, 1)).astype(np.uint16)


def unstriped(offs):
    return offs[:16].T.reshape(-1).astype(np.int64)


def striped8(idx):
    return np.asarray(idx).reshape(8, -1, 16).transpose(0, 2, 1).reshape(128, -1).astype(np.uint16)


def unstriped8(offs):
    return offs.reshape(8, 16, -1).transpose(0, 2, 1).reshape(8, -1).astype(np.int64)


def pick8(x, idx, run):
    r = np.arange(len(x))
    return x[r[:, None], idx[r % (8 * run) // run]]


K, J, N, T, V = 256, 1024, 256, 2048, 2048


def setup_inputs():
    n = np.random.standard_normal
    idx = np.stack([np.random.permutation(T)[:J] for _ in range(8)])
    idx2 = np.random.permutation(V)[:J]
    fj = mx_kscale(J)
    return {
        "xf": (n((K, T))).astype(np.float32),
        "ra": (np.random.uniform(0.5, 1.5, (1, J)) * fj).astype(np.float32),
        "gt": (n((N, V)) * np.exp(0.5 * n((1, V)))).astype(np.float32),
        "rb": (np.random.uniform(0.5, 1.5, (1, J)) / fj).astype(np.float32),
        "cp": (np.random.uniform(0.4, 1.2, (N, 1))).astype(np.float32),
        "old": (12.0 * n((K, N))).astype(np.float32),
        "offs": striped8(idx),
        "offs2": striped(idx2),
    }


def reference(xf, ra, gt, rb, cp, old, offs, offs2):
    idx = unstriped8(offs)
    idx2 = unstriped(offs2)
    us = pick8(f64(xf), idx, 16) * f64(ra)
    uj = us.T
    gs = np.minimum(f64(gt)[:, idx2], f64(cp)) * f64(rb)
    gj = gs.T
    ujq = mxq(uj, 0, "e4m3")
    gjq = mxq(gj, 0, "e5m2")
    w = ujq.T @ gjq
    y = 0.04 * np.maximum(w, f64(old))
    return y

@@ -1,0 +1,178 @@
+from contextlib import ExitStack
+
+import concourse.mybir as mybir
+from concourse.masks import make_identity
+
+K, J, N, T = 256, 1024, 256, 2048
+FLOPS = 2 * K * J * N
+
+F32 = mybir.dt.float32
+BF16 = mybir.dt.bfloat16
+U32 = mybir.dt.uint32
+U16 = mybir.dt.uint16
+U8 = mybir.dt.uint8
+E4M3 = mybir.dt.float8_e4m3fn_x4
+E5M2 = mybir.dt.float8_e5m2_x4
+ALU = mybir.AluOpType
+COPY = mybir.ActivationFunctionType.Copy
+
+P = 128
+PASS = 512
+GAIN = 0.04
+RA_ROW, RB_ROW, CP_ROW = 24, 56, 126
+
+
+def tile_list_moment_headpicks_bounded_larger_kernel(tc, xf, ra, gt, rb, cp, old, offs, offs2, out):
+    nc = tc.nc
+    with ExitStack() as ctx:
+        keep = ctx.enter_context(tc.tile_pool(name="keep", bufs=1))
+        psum = ctx.enter_context(tc.psum_pool(name="psum", bufs=1))
+
+        def sb(shape, dtype, name, tag=None):
+            return keep.tile(shape, dtype, name=name, tag=tag or name, align_bytes=64)
+
+        def bank(shape, name, tag):
+            return psum.tile(shape, F32, name=name, tag=tag)
+
+        x_list = keep.tile([P, J // 16], U16, name="x_list")
+        g_list = keep.tile([P, J // 16], U16, name="g_list")
+        g_win = [sb([P, T], F32, "g_win%d" % h) for h in range(2)]
+        x_win = [sb([P, T], F32, "x_win%d" % h) for h in range(2)]
+        old_sb = sb([P, 2, N], F32, "old_sb")
+        rows = sb([P, P], F32, "rows")
+        nc.sync.dma_start(rows[RB_ROW : RB_ROW + 8, :], rb.rearrange("o (m p) -> (o m) p", p=P))
+        nc.sync.dma_start(rows[RA_ROW : RA_ROW + 8, :], ra.rearrange("o (m p) -> (o m) p", p=P))
+        nc.sync.dma_start(rows[CP_ROW : CP_ROW + 2, :], cp.rearrange("(m p) o -> m (p o)", p=P))
+        nc.sync.dma_start(g_win[0][:], gt[0:P, :])
+        nc.sync.dma_start(g_list[:], offs2)
+        nc.sync.dma_start(g_win[1][:], gt[P : 2 * P, :])
+        nc.sync.dma_start(x_list[:], offs)
+        nc.sync.dma_start(x_win[0][:], xf[0:P, :])
+        nc.sync.dma_start(x_win[1][:], xf[P : 2 * P, :])
+        nc.sync.dma_start(old_sb[:], old.rearrange("(h p) n -> p h n", p=P))
+
+        nc.vector.memset(rows[0:RA_ROW, :], 0.0)
+        nc.vector.memset(rows[32:RB_ROW, :], 0.0)
+        nc.vector.memset(rows[64:CP_ROW, :], 0.0)
+        ident = sb([P, P], F32, "ident")
+        make_identity(nc, ident[:])
+
+        cols_ps = bank([P, P], "cols_ps", "b0")
+        nc.tensor.transpose(cols_ps[:], rows[:], ident[:])
+        cols = sb([P, P], F32, "cols")
+        nc.vector.tensor_copy(cols[:], cols_ps[:])
+
+        def spread(first_col, name, tag):
+            wide = bank([P, PASS], name, tag)
+            for m in range(4):
+                col = cols[:, first_col + m : first_col + m + 1]
+                nc.tensor.transpose(wide[:, m * P : (m + 1) * P], col.to_broadcast([P, P]), ident[:])
+            return wide
+
+        rb_ps = [spread(RB_ROW + 4 * a, "rb_ps%d" % a, "b%d" % (2 + a)) for a in range(2)]
+        ra0_ps = spread(RA_ROW, "ra0_ps", "b1")
+        ra1_ps = spread(RA_ROW + 4, "ra1_ps", "b4")
+        ra0_sb = sb([P, PASS], F32, "ra0_sb")
+
+        def listed(window, offsets, lo, hi):
+            return window[:].indirect(offsets[:, lo // 16 : hi // 16])
+
+        g_in = sb([P, 2, 2, P, 4], BF16, "g_in")
+        g_codes = sb([P, 2, N], U32, "g_codes")
+        g_scales = sb([P, 2, N], U8, "g_scales")
+
+        def g_values(h, vector_share, tag):
+            picked = sb([P, J], F32, "g_picked%d" % h)
+            nc.vector.tensor_copy(picked[:, 0:vector_share], listed(g_win[h], g_list, 0, vector_share))
+            for lo, hi in ((vector_share, PASS), (PASS, J)):
+                if lo < hi:
+                    nc.scalar.activation(picked[:, lo:hi], listed(g_win[h], g_list, lo, hi), COPY)
+            vals = sb([P, J], BF16, "g_vals%d" % h)
+            turned = bank([P, 2, 2, P], "g_turned%d" % h, tag)
+            words = vals[:].bitcast(F32)
+            for a in range(2):
+                span = slice(a * PASS, (a + 1) * PASS)
+                nc.vector.scalar_tensor_tensor(
+                    vals[:, span], picked[:, span], cols[:, CP_ROW + h : CP_ROW + h + 1], rb_ps[a][:],
+                    ALU.min, ALU.mult,
+                )
+                for u in range(2):
+                    nc.tensor.transpose(turned[:, a, u, :], words[:, 256 * a + u : 256 * (a + 1) : 2], ident[:])
+            return turned
+
+        def g_weave(h, turned, copy):
+            dst = g_in[:].rearrange("p a h c t -> p (a h c t)").bitcast(F32)
+            dst = dst.rearrange("p (a h c u) -> p a h c u", a=2, h=2, u=2)[:, :, h, :, :]
+            copy(dst, turned[:].rearrange("p a u c -> p a c u"))
+
+        def x_values(h, dsts, picked_tag, product_tag):
+            product = sb([P, PASS], F32, "x_product%d" % h, product_tag)
+            nc.vector.tensor_tensor(product[:], listed(x_win[h], x_list, 0, PASS), ra0_sb[:], ALU.mult)
+            picked = sb([P, PASS], F32, "x_picked%d" % h, picked_tag)
+            nc.scalar.activation(picked[:], listed(x_win[h], x_list, PASS, J), COPY)
+            vals = [sb([P, 2, P, 2], BF16, "x_vals%d_%d" % (h, a)) for a in range(2)]
+            order = "q (p u e) -> q u p e"
+            nc.vector.tensor_tensor(
+                vals[1][:], picked[:].rearrange(order, u=2, e=2), ra1_ps[:].rearrange(order, u=2, e=2), ALU.mult
+            )
+            nc.scalar.activation(vals[0][:], product[:].rearrange(order, u=2, e=2), COPY)
+            for a in (1, 0):
+                words = vals[a][:].rearrange("q u p e -> q (u p e)").bitcast(F32)
+                for u in range(2):
+                    nc.tensor.transpose(dsts[a][:, u, :], words[:, u * P : (u + 1) * P], ident[:])
+
+        def weave(dst, turned, copy):
+            words = dst.rearrange("p c t -> p (c t)").bitcast(F32).rearrange("p (c u) -> p c u", u=2)
+            copy(words, turned.rearrange("p u c -> p c u"))
+
+        g_turned0 = g_values(0, PASS, "b0")
+        nc.scalar.copy(ra0_sb[:], ra0_ps[:])
+        g_turned1 = g_values(1, 256, "b1")
+        g_weave(0, g_turned0, nc.vector.tensor_copy)
+
+        x_turned0 = bank([P, 2, 2, P], "x_turned0", "b5")
+        x_values(0, [x_turned0[:, a, :, :] for a in range(2)], "x_picked0", "x_product0")
+        g_weave(1, g_turned1, nc.scalar.copy)
+        for a in range(2):
+            nc.vector.quantize_mx(
+                g_codes[:, a, :].bitcast(E5M2), g_scales[:, a, :],
+                g_in[:, a, :, :, :].rearrange("p h c t -> p (h c t)"),
+            )
+
+        x_turned1 = [bank([P, 2, P], "x_turned1_%d" % a, "b%d" % (6 + a)) for a in range(2)]
+        x_values(1, [x_turned1[a][:] for a in range(2)], "late_v", "late_s")
+
+        x_codes = [sb([P, 2, P], U32, "x_codes%d" % h) for h in range(2)]
+        x_scales = [sb([P, 2, P], U8, "x_scales%d" % h) for h in range(2)]
+        x_in0 = sb([P, 2, P, 4], BF16, "x_in0", "late_v")
+        x0_words = x_in0[:].rearrange("p a c t -> p (a c t)").bitcast(F32).rearrange("p (a c u) -> p a c u", a=2, u=2)
+        nc.vector.tensor_copy(x0_words, x_turned0[:].rearrange("p a u c -> p a c u"))
+        old_scaled = sb([P, 2, N], F32, "old_scaled", "late_s")
+        nc.scalar.mul(old_scaled[:], old_sb[:], GAIN)
+        nc.vector.quantize_mx(
+            x_codes[0][:].rearrange("p a c -> p (a c)").bitcast(E4M3),
+            x_scales[0][:].rearrange("p a c -> p (a c)"),
+            x_in0[:].rearrange("p a c t -> p (a c t)"),
+        )
+
+        def product_pass(acc, h, a, first):
+            nc.tensor.matmul_mx(
+                acc[:], x_codes[h][:, a, :].bitcast(E4M3), x_scales[h][:, a, :],
+                g_codes[:, a, :].bitcast(E5M2), g_scales[:, a, :], start=first, stop=not first,
+            )
+
+        accs = [bank([P, N], "acc%d" % h, "b%d" % (2 + h)) for h in range(2)]
+        x_in1 = [sb([P, P, 4], BF16, "x_in1_%d" % a) for a in range(2)]
+        weave(x_in1[1][:], x_turned1[1][:], nc.vector.tensor_copy)
+        weave(x_in1[0][:], x_turned1[0][:], nc.scalar.copy)
+        for a in range(2):
+            product_pass(accs[0], 0, a, a == 0)
+        for a in (1, 0):
+            nc.vector.quantize_mx(
+                x_codes[1][:, a, :].bitcast(E4M3), x_scales[1][:, a, :], x_in1[a][:].rearrange("p c t -> p (c t)")
+            )
+            product_pass(accs[1], 1, a, a == 1)
+        for h in range(2):
+            result = sb([P, N], F32, "result%d" % h)
+            nc.vector.scalar_tensor_tensor(result[:], accs[h][:], GAIN, old_scaled[:, h, :], ALU.mult, ALU.max)
+            nc.sync.dma_start(out[h * P : (h + 1) * P, :], result[:])

@@ -18,6 +18,7 @@ COPY = mybir.ActivationFunctionType.Copy
 
 P = 128
 PASS = 512
+HALF = PASS // 2
 GAIN = 0.04
 RA_ROW, RB_ROW, CP_ROW = 24, 56, 126
 
@@ -39,7 +40,7 @@ def tile_list_moment_headpicks_bounded_larger_kernel(tc, xf, ra, gt, rb, cp, old
         g_win = [sb([P, T], F32, "g_win%d" % h) for h in range(2)]
         x_win = [sb([P, T], F32, "x_win%d" % h) for h in range(2)]
         old_sb = sb([P, 2, N], F32, "old_sb")
-        rows = sb([P, P], F32, "rows")
+        rows = sb([P, P], F32, "rows", "g_front0")
         nc.sync.dma_start(rows[RB_ROW : RB_ROW + 8, :], rb.rearrange("o (m p) -> (o m) p", p=P))
         nc.sync.dma_start(rows[RA_ROW : RA_ROW + 8, :], ra.rearrange("o (m p) -> (o m) p", p=P))
         nc.sync.dma_start(rows[CP_ROW : CP_ROW + 2, :], cp.rearrange("(m p) o -> m (p o)", p=P))
@@ -70,89 +71,88 @@ def tile_list_moment_headpicks_bounded_larger_kernel(tc, xf, ra, gt, rb, cp, old
             return wide
 
         rb_ps = [spread(RB_ROW + 4 * a, "rb_ps%d" % a, "b%d" % (2 + a)) for a in range(2)]
-        ra0_ps = spread(RA_ROW, "ra0_ps", "b1")
-        ra1_ps = spread(RA_ROW + 4, "ra1_ps", "b4")
-        ra0_sb = sb([P, PASS], F32, "ra0_sb")
+        ra_ps = [spread(RA_ROW + 4 * a, "ra_ps%d" % a, ("b1", "b4")[a]) for a in range(2)]
 
         def listed(window, offsets, lo, hi):
             return window[:].indirect(offsets[:, lo // 16 : hi // 16])
 
-        g_in = sb([P, 2, 2, P, 4], BF16, "g_in")
-        g_codes = sb([P, 2, N], U32, "g_codes")
-        g_scales = sb([P, 2, N], U8, "g_scales")
+        def turn(vals, dst):
+            for u in range(2):
+                nc.tensor.transpose(dst[:, u, :], vals[:].bitcast(F32)[:, u : 2 * P : 2], ident[:])
 
-        def g_values(h, vector_share, tag):
-            picked = sb([P, J], F32, "g_picked%d" % h)
-            nc.vector.tensor_copy(picked[:, 0:vector_share], listed(g_win[h], g_list, 0, vector_share))
-            for lo, hi in ((vector_share, PASS), (PASS, J)):
-                if lo < hi:
-                    nc.scalar.activation(picked[:, lo:hi], listed(g_win[h], g_list, lo, hi), COPY)
-            vals = sb([P, J], BF16, "g_vals%d" % h)
+        def g_values(h, tag):
+            front = sb([P, PASS], F32, "g_front%d" % h)
+            nc.vector.tensor_copy(front[:], listed(g_win[h], g_list, 0, PASS))
+            back = [sb([P, HALF], F32, "g_back%d_%d" % (h, b)) for b in range(2)]
+            for b in range(2):
+                lo = PASS + b * HALF
+                nc.scalar.activation(back[b][:], listed(g_win[h], g_list, lo, lo + HALF), COPY)
+            vals = [sb([P, PASS], BF16, "g_vals%d_%d" % (h, a)) for a in range(2)]
+            bound = cols[:, CP_ROW + h : CP_ROW + h + 1]
+            for dst, src, weight in (
+                (vals[1][:, :HALF], back[0][:], rb_ps[1][:, :HALF]),
+                (vals[0][:], front[:], rb_ps[0][:]),
+                (vals[1][:, HALF:], back[1][:], rb_ps[1][:, HALF:]),
+            ):
+                nc.vector.scalar_tensor_tensor(dst, src, bound, weight, ALU.min, ALU.mult)
             turned = bank([P, 2, 2, P], "g_turned%d" % h, tag)
-            words = vals[:].bitcast(F32)
             for a in range(2):
-                span = slice(a * PASS, (a + 1) * PASS)
-                nc.vector.scalar_tensor_tensor(
-                    vals[:, span], picked[:, span], cols[:, CP_ROW + h : CP_ROW + h + 1], rb_ps[a][:],
-                    ALU.min, ALU.mult,
-                )
-                for u in range(2):
-                    nc.tensor.transpose(turned[:, a, u, :], words[:, 256 * a + u : 256 * (a + 1) : 2], ident[:])
+                turn(vals[a], turned[:, a, :, :])
             return turned
 
-        def g_weave(h, turned, copy):
-            dst = g_in[:].rearrange("p a h c t -> p (a h c t)").bitcast(F32)
-            dst = dst.rearrange("p (a h c u) -> p a h c u", a=2, h=2, u=2)[:, :, h, :, :]
-            copy(dst, turned[:].rearrange("p a u c -> p a c u"))
-
-        def x_values(h, dsts, picked_tag, product_tag):
-            product = sb([P, PASS], F32, "x_product%d" % h, product_tag)
+        def x_values(h, cast):
+            product = sb([P, PASS], F32, "x_product%d" % h)
             nc.vector.tensor_tensor(product[:], listed(x_win[h], x_list, 0, PASS), ra0_sb[:], ALU.mult)
-            picked = sb([P, PASS], F32, "x_picked%d" % h, picked_tag)
+            picked = sb([P, PASS], F32, "x_picked%d" % h)
             nc.scalar.activation(picked[:], listed(x_win[h], x_list, PASS, J), COPY)
-            vals = [sb([P, 2, P, 2], BF16, "x_vals%d_%d" % (h, a)) for a in range(2)]
-            order = "q (p u e) -> q u p e"
-            nc.vector.tensor_tensor(
-                vals[1][:], picked[:].rearrange(order, u=2, e=2), ra1_ps[:].rearrange(order, u=2, e=2), ALU.mult
-            )
-            nc.scalar.activation(vals[0][:], product[:].rearrange(order, u=2, e=2), COPY)
-            for a in (1, 0):
-                words = vals[a][:].rearrange("q u p e -> q (u p e)").bitcast(F32)
-                for u in range(2):
-                    nc.tensor.transpose(dsts[a][:, u, :], words[:, u * P : (u + 1) * P], ident[:])
+            vals = [sb([P, PASS], BF16, "x_vals%d_%d" % (h, a)) for a in range(2)]
+            nc.vector.tensor_tensor(vals[1][:], picked[:], ra_ps[1][:], ALU.mult)
+            cast(vals[0][:], product[:])
+            return vals
 
-        def weave(dst, turned, copy):
-            words = dst.rearrange("p c t -> p (c t)").bitcast(F32).rearrange("p (c u) -> p c u", u=2)
-            copy(words, turned.rearrange("p u c -> p c u"))
+        def weave(woven, turned):
+            words = woven.bitcast(F32).rearrange("p (a c u) -> p a c u", a=2, u=2)
+            nc.scalar.copy(words, turned[:].rearrange("p a u c -> p a c u"))
 
-        g_turned0 = g_values(0, PASS, "b0")
-        nc.scalar.copy(ra0_sb[:], ra0_ps[:])
-        g_turned1 = g_values(1, 256, "b1")
-        g_weave(0, g_turned0, nc.vector.tensor_copy)
+        def pool_cast(dst, src):
+            nc.gpsimd.tensor_scalar(dst, src, 1.0, 0.0, ALU.mult, ALU.add)
 
-        x_turned0 = bank([P, 2, 2, P], "x_turned0", "b5")
-        x_values(0, [x_turned0[:, a, :, :] for a in range(2)], "x_picked0", "x_product0")
-        g_weave(1, g_turned1, nc.scalar.copy)
+        g_turned0 = g_values(0, "b0")
+        ra0_sb = sb([P, PASS], F32, "ra0_sb", "g_back0_0")
+        nc.scalar.copy(ra0_sb[:], ra_ps[0][:])
+        g_turned1 = g_values(1, "b5")
+        g_in0 = sb([P, J], BF16, "g_in0", "g_back1_0")
+        weave(g_in0[:], g_turned0)
+
+        x_turned0 = bank([P, 2, 2, P], "x_turned0", "b6")
+        vals = x_values(0, nc.scalar.copy)
         for a in range(2):
-            nc.vector.quantize_mx(
-                g_codes[:, a, :].bitcast(E5M2), g_scales[:, a, :],
-                g_in[:, a, :, :, :].rearrange("p h c t -> p (h c t)"),
-            )
+            turn(vals[a], x_turned0[:, a, :, :])
 
-        x_turned1 = [bank([P, 2, P], "x_turned1_%d" % a, "b%d" % (6 + a)) for a in range(2)]
-        x_values(1, [x_turned1[a][:] for a in range(2)], "late_v", "late_s")
+        x_turned1 = [bank([P, 2, P], "x_turned1_%d" % a, ("b0", "b7")[a]) for a in range(2)]
+        vals = x_values(1, pool_cast)
+        for a in (1, 0):
+            turn(vals[a], x_turned1[a][:])
+
+        late_in = sb([P, 2 * J], BF16, "late_in", "g_back0_0")
+        weave(late_in[:, :J], g_turned1)
+        weave(late_in[:, J:], x_turned0)
+        g_in = [g_in0[:], late_in[:, :J]]
+        g_codes = sb([P, 2, N], U32, "g_codes", "x_picked1")
+        g_scales = sb([P, 2, N], U8, "g_scales")
+        for h in range(2):
+            for a in range(2):
+                span = slice(h * P, (h + 1) * P)
+                nc.vector.quantize_mx(
+                    g_codes[:, a, span].bitcast(E5M2), g_scales[:, a, span], g_in[h][:, a * PASS : (a + 1) * PASS]
+                )
 
         x_codes = [sb([P, 2, P], U32, "x_codes%d" % h) for h in range(2)]
         x_scales = [sb([P, 2, P], U8, "x_scales%d" % h) for h in range(2)]
-        x_in0 = sb([P, 2, P, 4], BF16, "x_in0", "late_v")
-        x0_words = x_in0[:].rearrange("p a c t -> p (a c t)").bitcast(F32).rearrange("p (a c u) -> p a c u", a=2, u=2)
-        nc.vector.tensor_copy(x0_words, x_turned0[:].rearrange("p a u c -> p a c u"))
-        old_scaled = sb([P, 2, N], F32, "old_scaled", "late_s")
-        nc.scalar.mul(old_scaled[:], old_sb[:], GAIN)
         nc.vector.quantize_mx(
             x_codes[0][:].rearrange("p a c -> p (a c)").bitcast(E4M3),
             x_scales[0][:].rearrange("p a c -> p (a c)"),
-            x_in0[:].rearrange("p a c t -> p (a c t)"),
+            late_in[:, J:],
         )
 
         def product_pass(acc, h, a, first):
@@ -162,16 +162,16 @@ def tile_list_moment_headpicks_bounded_larger_kernel(tc, xf, ra, gt, rb, cp, old
             )
 
         accs = [bank([P, N], "acc%d" % h, "b%d" % (2 + h)) for h in range(2)]
-        x_in1 = [sb([P, P, 4], BF16, "x_in1_%d" % a) for a in range(2)]
-        weave(x_in1[1][:], x_turned1[1][:], nc.vector.tensor_copy)
-        weave(x_in1[0][:], x_turned1[0][:], nc.scalar.copy)
         for a in range(2):
             product_pass(accs[0], 0, a, a == 0)
         for a in (1, 0):
-            nc.vector.quantize_mx(
-                x_codes[1][:, a, :].bitcast(E4M3), x_scales[1][:, a, :], x_in1[a][:].rearrange("p c t -> p (c t)")
-            )
+            woven = sb([P, P * 4], BF16, "x_in1_%d" % a)
+            words = woven[:].bitcast(F32).rearrange("p (c u) -> p c u", u=2)
+            nc.scalar.copy(words, x_turned1[a][:].rearrange("p u c -> p c u"))
+            nc.vector.quantize_mx(x_codes[1][:, a, :].bitcast(E4M3), x_scales[1][:, a, :], woven[:])
             product_pass(accs[1], 1, a, a == 1)
+        old_scaled = sb([P, 2, N], F32, "old_scaled", "x_vals1_0")
+        nc.scalar.mul(old_scaled[:], old_sb[:], GAIN)
         for h in range(2):
             result = sb([P, N], F32, "result%d" % h)
             nc.vector.scalar_tensor_tensor(result[:], accs[h][:], GAIN, old_scaled[:, h, :], ALU.mult, ALU.max)

@@ -20,7 +20,7 @@ P = 128
 PASS = 512
 HALF = PASS // 2
 GAIN = 0.04
-RA_ROW, RB_ROW, CP_ROW = 24, 56, 126
+RA_ROW, CP_ROW, RB_ROW = 24, 54, 56
 
 
 def tile_list_moment_headpicks_bounded_larger_kernel(tc, xf, ra, gt, rb, cp, old, offs, offs2, out):
@@ -40,7 +40,8 @@ def tile_list_moment_headpicks_bounded_larger_kernel(tc, xf, ra, gt, rb, cp, old
         g_win = [sb([P, T], F32, "g_win%d" % h) for h in range(2)]
         x_win = [sb([P, T], F32, "x_win%d" % h) for h in range(2)]
         old_sb = sb([P, 2, N], F32, "old_sb")
-        rows = sb([P, P], F32, "rows", "g_front0")
+        rows = sb([P, P], F32, "rows", "front")
+        ra_back = sb([P, 4], F32, "ra_back")
         nc.sync.dma_start(rows[RB_ROW : RB_ROW + 8, :], rb.rearrange("o (m p) -> (o m) p", p=P))
         nc.sync.dma_start(rows[RA_ROW : RA_ROW + 8, :], ra.rearrange("o (m p) -> (o m) p", p=P))
         nc.sync.dma_start(rows[CP_ROW : CP_ROW + 2, :], cp.rearrange("(m p) o -> m (p o)", p=P))
@@ -50,129 +51,148 @@ def tile_list_moment_headpicks_bounded_larger_kernel(tc, xf, ra, gt, rb, cp, old
         nc.sync.dma_start(x_list[:], offs)
         nc.sync.dma_start(x_win[0][:], xf[0:P, :])
         nc.sync.dma_start(x_win[1][:], xf[P : 2 * P, :])
+        nc.sync.dma_start(ra_back[:], ra[:, PASS:].rearrange("o (p t) -> (o p) t", t=4))
         nc.sync.dma_start(old_sb[:], old.rearrange("(h p) n -> p h n", p=P))
 
         nc.vector.memset(rows[0:RA_ROW, :], 0.0)
-        nc.vector.memset(rows[32:RB_ROW, :], 0.0)
-        nc.vector.memset(rows[64:CP_ROW, :], 0.0)
+        nc.vector.memset(rows[32:CP_ROW, :], 0.0)
+        zero = sb([P, 1], F32, "zero")
+        nc.vector.memset(zero[64:P, :], 0.0)
+        nc.scalar.activation(rows[64:P, :], zero[64:P, :].to_broadcast([P - 64, P]), COPY)
         ident = sb([P, P], F32, "ident")
         make_identity(nc, ident[:])
 
         cols_ps = bank([P, P], "cols_ps", "b0")
         nc.tensor.transpose(cols_ps[:], rows[:], ident[:])
-        cols = sb([P, P], F32, "cols")
-        nc.vector.tensor_copy(cols[:], cols_ps[:])
+        cols = sb([P, 64 - RA_ROW], F32, "cols")
+        nc.vector.tensor_copy(cols[:], cols_ps[:, RA_ROW:64])
 
-        def spread(first_col, name, tag):
+        def spread(source, first_col, name, tag):
             wide = bank([P, PASS], name, tag)
             for m in range(4):
-                col = cols[:, first_col + m : first_col + m + 1]
+                col = source[:, first_col + m : first_col + m + 1]
                 nc.tensor.transpose(wide[:, m * P : (m + 1) * P], col.to_broadcast([P, P]), ident[:])
             return wide
 
-        rb_ps = [spread(RB_ROW + 4 * a, "rb_ps%d" % a, "b%d" % (2 + a)) for a in range(2)]
-        ra_ps = [spread(RA_ROW + 4 * a, "ra_ps%d" % a, ("b1", "b4")[a]) for a in range(2)]
+        rb_ps = {a: spread(cols, RB_ROW - RA_ROW + 4 * a, "rb_ps%d" % a, "b%d" % (2 + a)) for a in (1, 0)}
+        ra_ps = [spread(cols, 4 * a, "ra_ps%d" % a, ("b1", "b4")[a]) for a in range(2)]
 
         def listed(window, offsets, lo, hi):
             return window[:].indirect(offsets[:, lo // 16 : hi // 16])
 
         def turn(vals, dst):
             for u in range(2):
-                nc.tensor.transpose(dst[:, u, :], vals[:].bitcast(F32)[:, u : 2 * P : 2], ident[:])
+                nc.tensor.transpose(dst[:, u, :], vals.bitcast(F32)[:, u : 2 * P : 2], ident[:])
 
-        def g_values(h, tag):
-            front = sb([P, PASS], F32, "g_front%d" % h)
-            nc.vector.tensor_copy(front[:], listed(g_win[h], g_list, 0, PASS))
-            back = [sb([P, HALF], F32, "g_back%d_%d" % (h, b)) for b in range(2)]
+        def g_values(h, tag, front, back):
+            nc.vector.tensor_copy(front, listed(g_win[h], g_list, 0, PASS))
             for b in range(2):
                 lo = PASS + b * HALF
-                nc.scalar.activation(back[b][:], listed(g_win[h], g_list, lo, lo + HALF), COPY)
+                nc.scalar.activation(back[b], listed(g_win[h], g_list, lo, lo + HALF), COPY)
             vals = [sb([P, PASS], BF16, "g_vals%d_%d" % (h, a)) for a in range(2)]
-            bound = cols[:, CP_ROW + h : CP_ROW + h + 1]
+            bound = cols[:, CP_ROW - RA_ROW + h : CP_ROW - RA_ROW + h + 1]
             for dst, src, weight in (
-                (vals[1][:, :HALF], back[0][:], rb_ps[1][:, :HALF]),
-                (vals[0][:], front[:], rb_ps[0][:]),
-                (vals[1][:, HALF:], back[1][:], rb_ps[1][:, HALF:]),
+                (vals[1][:, :HALF], back[0], rb_ps[1][:, :HALF]),
+                (vals[0][:], front, rb_ps[0][:]),
+                (vals[1][:, HALF:], back[1], rb_ps[1][:, HALF:]),
             ):
                 nc.vector.scalar_tensor_tensor(dst, src, bound, weight, ALU.min, ALU.mult)
             turned = bank([P, 2, 2, P], "g_turned%d" % h, tag)
             for a in range(2):
-                turn(vals[a], turned[:, a, :, :])
+                turn(vals[a][:], turned[:, a, :, :])
             return turned
 
-        def x_values(h, cast):
-            product = sb([P, PASS], F32, "x_product%d" % h)
-            nc.vector.tensor_tensor(product[:], listed(x_win[h], x_list, 0, PASS), ra0_sb[:], ALU.mult)
-            picked = sb([P, PASS], F32, "x_picked%d" % h)
-            nc.scalar.activation(picked[:], listed(x_win[h], x_list, PASS, J), COPY)
-            vals = [sb([P, PASS], BF16, "x_vals%d_%d" % (h, a)) for a in range(2)]
-            nc.vector.tensor_tensor(vals[1][:], picked[:], ra_ps[1][:], ALU.mult)
-            cast(vals[0][:], product[:])
-            return vals
+        def x_gather(h, product, picked):
+            nc.vector.tensor_tensor(product, listed(x_win[h], x_list, 0, PASS), ra0_sb[:], ALU.mult)
+            nc.scalar.activation(picked, listed(x_win[h], x_list, PASS, J), COPY)
 
         def weave(woven, turned):
             words = woven.bitcast(F32).rearrange("p (a c u) -> p a c u", a=2, u=2)
             nc.scalar.copy(words, turned[:].rearrange("p a u c -> p a c u"))
 
-        def pool_cast(dst, src):
-            nc.gpsimd.tensor_scalar(dst, src, 1.0, 0.0, ALU.mult, ALU.add)
-
-        g_turned0 = g_values(0, "b0")
-        ra0_sb = sb([P, PASS], F32, "ra0_sb", "g_back0_0")
+        front0 = sb([P, PASS], F32, "g_front0", "front")
+        back0 = [sb([P, HALF], F32, "g_back0_%d" % b, "back%d" % b) for b in range(2)]
+        g_turned0 = g_values(0, "b0", front0[:], [back0[0][:], back0[1][:]])
+        ra0_sb = sb([P, PASS], F32, "ra0_sb", "back0")
         nc.scalar.copy(ra0_sb[:], ra_ps[0][:])
-        g_turned1 = g_values(1, "b5")
-        g_in0 = sb([P, J], BF16, "g_in0", "g_back1_0")
-        weave(g_in0[:], g_turned0)
+        front1 = sb([P, PASS + HALF], F32, "g_front1", "front")
+        back1 = sb([P, HALF], F32, "g_back1", "back1")
+        g_turned1 = g_values(1, "b5", front1[:, :PASS], [front1[:, PASS:], back1[:]])
 
-        x_turned0 = bank([P, 2, 2, P], "x_turned0", "b6")
-        vals = x_values(0, nc.scalar.copy)
-        for a in range(2):
-            turn(vals[a], x_turned0[:, a, :, :])
+        x_turned0 = [bank([P, 4, P], "x_turned0_%d" % a, ("b1", "b6")[a]) for a in range(2)]
+        x0 = [sb([P, PASS], F32, "x_product0", "front"), sb([P, PASS], F32, "x_picked0", "g_vals0_1")]
+        x_gather(0, x0[0][:], x0[1][:])
+        for a in (1, 0):
+            for t in range(4):
+                nc.tensor.transpose(x_turned0[a][:, t, :], x0[a][:, t:PASS:4], ident[:])
+
+        shared = sb([P, 2 * PASS], F32, "shared", "g_vals1_1")
+        g_in0, picked = shared[:, :PASS].bitcast(BF16), shared[:, PASS:]
+        weave(g_in0, g_turned0)
 
         x_turned1 = [bank([P, 2, P], "x_turned1_%d" % a, ("b0", "b7")[a]) for a in range(2)]
-        vals = x_values(1, pool_cast)
-        for a in (1, 0):
+        product = sb([P, PASS], F32, "x_product1", "back1")
+        x_gather(1, product[:], picked)
+        late_in = sb([P, 2 * J + PASS], BF16, "late_in", "back0")
+        x_in0 = late_in[:, J : 2 * J].rearrange("p (a c t) -> p a c t", a=2, t=4)
+
+        def weigh_turned(lo, hi):
+            nc.vector.tensor_tensor(
+                x_in0[:, 1, lo:hi, :], x_turned0[1][:, :, lo:hi].rearrange("p t c -> p c t"),
+                ra_back[:].unsqueeze(1).to_broadcast([P, hi - lo, 4]), ALU.mult,
+            )
+
+        rounded = sb([P, PASS], BF16, "x_vals1_0")
+        vals = [rounded[:], late_in[:, 2 * J :]]
+        nc.gpsimd.tensor_scalar(vals[0], product[:], 1.0, 0.0, ALU.mult, ALU.add)
+        weigh_turned(0, P // 2)
+        nc.vector.tensor_tensor(vals[1], picked, ra_ps[1][:], ALU.mult)
+        weigh_turned(P // 2, P)
+        for a in range(2):
             turn(vals[a], x_turned1[a][:])
 
-        late_in = sb([P, 2 * J], BF16, "late_in", "g_back0_0")
+        nc.scalar.copy(x_in0[:, 0, :, :], x_turned0[0][:].rearrange("p t c -> p c t"))
         weave(late_in[:, :J], g_turned1)
-        weave(late_in[:, J:], x_turned0)
-        g_in = [g_in0[:], late_in[:, :J]]
-        g_codes = sb([P, 2, N], U32, "g_codes", "x_picked1")
-        g_scales = sb([P, 2, N], U8, "g_scales")
-        for h in range(2):
-            for a in range(2):
-                span = slice(h * P, (h + 1) * P)
-                nc.vector.quantize_mx(
-                    g_codes[:, a, span].bitcast(E5M2), g_scales[:, a, span], g_in[h][:, a * PASS : (a + 1) * PASS]
-                )
-
+        g_in = [g_in0, late_in[:, :J]]
+        g_codes = sb([P, 2, 2 * P], U32, "g_codes", "back1")
+        g_scales = sb([P, 2, 2 * P], U8, "g_scales")
+        nc.vector.quantize_mx(g_codes[:, 0, :].bitcast(E5M2), g_scales[:, 0, :], g_in[0])
         x_codes = [sb([P, 2, P], U32, "x_codes%d" % h) for h in range(2)]
         x_scales = [sb([P, 2, P], U8, "x_scales%d" % h) for h in range(2)]
         nc.vector.quantize_mx(
             x_codes[0][:].rearrange("p a c -> p (a c)").bitcast(E4M3),
             x_scales[0][:].rearrange("p a c -> p (a c)"),
-            late_in[:, J:],
+            late_in[:, J : 2 * J],
         )
+        nc.vector.quantize_mx(g_codes[:, 1, :].bitcast(E5M2), g_scales[:, 1, :], g_in[1])
 
-        def product_pass(acc, h, a, first):
+        def product_pass(acc, h, nh, a, first):
+            span = slice(a * P, (a + 1) * P)
             nc.tensor.matmul_mx(
-                acc[:], x_codes[h][:, a, :].bitcast(E4M3), x_scales[h][:, a, :],
-                g_codes[:, a, :].bitcast(E5M2), g_scales[:, a, :], start=first, stop=not first,
+                acc, x_codes[h][:, a, :].bitcast(E4M3), x_scales[h][:, a, :],
+                g_codes[:, nh, span].bitcast(E5M2), g_scales[:, nh, span], start=first, stop=not first,
             )
 
-        accs = [bank([P, N], "acc%d" % h, "b%d" % (2 + h)) for h in range(2)]
+        acc0 = bank([P, N], "acc0", "b2")
+        for nh in range(2):
+            for a in range(2):
+                product_pass(acc0[:, nh * P : (nh + 1) * P], 0, nh, a, a == 0)
+        acc1 = [bank([P, P], "acc1_%d" % nh, ("b3", "b4")[nh]) for nh in range(2)]
         for a in range(2):
-            product_pass(accs[0], 0, a, a == 0)
-        for a in (1, 0):
             woven = sb([P, P * 4], BF16, "x_in1_%d" % a)
             words = woven[:].bitcast(F32).rearrange("p (c u) -> p c u", u=2)
             nc.scalar.copy(words, x_turned1[a][:].rearrange("p u c -> p c u"))
             nc.vector.quantize_mx(x_codes[1][:, a, :].bitcast(E4M3), x_scales[1][:, a, :], woven[:])
-            product_pass(accs[1], 1, a, a == 1)
-        old_scaled = sb([P, 2, N], F32, "old_scaled", "x_vals1_0")
+            for nh in range(2):
+                product_pass(acc1[nh][:], 1, nh, a, a == 0)
+        old_scaled = sb([P, 2, N], F32, "old_scaled", "back0")
         nc.scalar.mul(old_scaled[:], old_sb[:], GAIN)
-        for h in range(2):
-            result = sb([P, N], F32, "result%d" % h)
-            nc.vector.scalar_tensor_tensor(result[:], accs[h][:], GAIN, old_scaled[:, h, :], ALU.mult, ALU.max)
-            nc.sync.dma_start(out[h * P : (h + 1) * P, :], result[:])
+
+        def finish(acc, h, lo, hi, queue):
+            result = sb([P, hi - lo], F32, "result%d_%d" % (h, lo))
+            nc.vector.scalar_tensor_tensor(result[:], acc, GAIN, old_scaled[:, h, lo:hi], ALU.mult, ALU.max)
+            queue.dma_start(out[h * P : (h + 1) * P, lo:hi], result[:])
+
+        finish(acc0[:], 0, 0, N, nc.sync)
+        finish(acc1[0][:], 1, 0, P, nc.scalar)
+        finish(acc1[1][:], 1, P, N, nc.sync)

@@ -19,8 +19,9 @@ COPY = mybir.ActivationFunctionType.Copy
 P = 128
 PASS = 512
 HALF = PASS // 2
+GROUP = 16
 GAIN = 0.04
-RA_ROW, CP_ROW, RB_ROW = 24, 54, 56
+RA_ROW, CP_ROW, RB_ROW, SPARE_ROW = 24, 54, 56, 64
 
 
 def tile_list_moment_headpicks_bounded_larger_kernel(tc, xf, ra, gt, rb, cp, old, offs, offs2, out):
@@ -35,18 +36,18 @@ def tile_list_moment_headpicks_bounded_larger_kernel(tc, xf, ra, gt, rb, cp, old
         def bank(shape, name, tag):
             return psum.tile(shape, F32, name=name, tag=tag)
 
-        x_list = keep.tile([P, J // 16], U16, name="x_list")
-        g_list = keep.tile([P, J // 16], U16, name="g_list")
+        x_list = keep.tile([P, J // GROUP], U16, name="x_list")
+        g_list = keep.tile([P, J // GROUP], U16, name="g_list")
         g_win = [sb([P, T], F32, "g_win%d" % h) for h in range(2)]
         x_win = [sb([P, T], F32, "x_win%d" % h) for h in range(2)]
         old_sb = sb([P, 2, N], F32, "old_sb")
         rows = sb([P, P], F32, "rows", "front")
         ra_back = sb([P, 4], F32, "ra_back")
-        nc.sync.dma_start(rows[RB_ROW : RB_ROW + 8, :], rb.rearrange("o (m p) -> (o m) p", p=P))
+        nc.scalar.dma_start(rows[RB_ROW : RB_ROW + 8, :], rb.rearrange("o (m p) -> (o m) p", p=P))
+        nc.scalar.dma_start(rows[CP_ROW : CP_ROW + 2, :], cp.rearrange("(m p) o -> m (p o)", p=P))
         nc.sync.dma_start(rows[RA_ROW : RA_ROW + 8, :], ra.rearrange("o (m p) -> (o m) p", p=P))
-        nc.sync.dma_start(rows[CP_ROW : CP_ROW + 2, :], cp.rearrange("(m p) o -> m (p o)", p=P))
-        nc.sync.dma_start(g_win[0][:], gt[0:P, :])
         nc.sync.dma_start(g_list[:], offs2)
+        nc.sync.dma_start(g_win[0][:], gt[0:P, :])
         nc.sync.dma_start(g_win[1][:], gt[P : 2 * P, :])
         nc.sync.dma_start(x_list[:], offs)
         nc.sync.dma_start(x_win[0][:], xf[0:P, :])
@@ -57,30 +58,30 @@ def tile_list_moment_headpicks_bounded_larger_kernel(tc, xf, ra, gt, rb, cp, old
         nc.vector.memset(rows[0:RA_ROW, :], 0.0)
         nc.vector.memset(rows[32:CP_ROW, :], 0.0)
         zero = sb([P, 1], F32, "zero")
-        nc.vector.memset(zero[64:P, :], 0.0)
-        nc.scalar.activation(rows[64:P, :], zero[64:P, :].to_broadcast([P - 64, P]), COPY)
+        nc.vector.memset(zero[SPARE_ROW:P, :], 0.0)
+        nc.scalar.activation(rows[SPARE_ROW:P, :], zero[SPARE_ROW:P, :].to_broadcast([P - SPARE_ROW, P]), COPY)
         ident = sb([P, P], F32, "ident")
         make_identity(nc, ident[:])
 
         cols_ps = bank([P, P], "cols_ps", "b0")
         nc.tensor.transpose(cols_ps[:], rows[:], ident[:])
-        cols = sb([P, 64 - RA_ROW], F32, "cols")
-        nc.vector.tensor_copy(cols[:], cols_ps[:, RA_ROW:64])
+        cols = sb([P, SPARE_ROW - RA_ROW], F32, "cols")
+        nc.vector.tensor_copy(cols[:], cols_ps[:, RA_ROW:SPARE_ROW])
 
-        def spread(source, first_col, name, tag):
+        def spread(first_col, name, tag):
             wide = bank([P, PASS], name, tag)
-            for m in range(4):
-                col = source[:, first_col + m : first_col + m + 1]
+            for m in range(PASS // P):
+                col = cols[:, first_col + m : first_col + m + 1]
                 nc.tensor.transpose(wide[:, m * P : (m + 1) * P], col.to_broadcast([P, P]), ident[:])
             return wide
 
-        rb_ps = {a: spread(cols, RB_ROW - RA_ROW + 4 * a, "rb_ps%d" % a, "b%d" % (2 + a)) for a in (1, 0)}
-        ra_ps = [spread(cols, 4 * a, "ra_ps%d" % a, ("b1", "b4")[a]) for a in range(2)]
+        rb_ps = {a: spread(RB_ROW - RA_ROW + 4 * a, "rb_ps%d" % a, "b%d" % (2 + a)) for a in (1, 0)}
+        ra_ps = [spread(4 * a, "ra_ps%d" % a, ("b1", "b4")[a]) for a in range(2)]
 
         def listed(window, offsets, lo, hi):
-            return window[:].indirect(offsets[:, lo // 16 : hi // 16])
+            return window[:].indirect(offsets[:, lo // GROUP : hi // GROUP])
 
-        def turn(vals, dst):
+        def turn_words(vals, dst):
             for u in range(2):
                 nc.tensor.transpose(dst[:, u, :], vals.bitcast(F32)[:, u : 2 * P : 2], ident[:])
 
@@ -99,7 +100,7 @@ def tile_list_moment_headpicks_bounded_larger_kernel(tc, xf, ra, gt, rb, cp, old
                 nc.vector.scalar_tensor_tensor(dst, src, bound, weight, ALU.min, ALU.mult)
             turned = bank([P, 2, 2, P], "g_turned%d" % h, tag)
             for a in range(2):
-                turn(vals[a][:], turned[:, a, :, :])
+                turn_words(vals[a][:], turned[:, a, :, :])
             return turned
 
         def x_gather(h, product, picked):
@@ -115,6 +116,7 @@ def tile_list_moment_headpicks_bounded_larger_kernel(tc, xf, ra, gt, rb, cp, old
         g_turned0 = g_values(0, "b0", front0[:], [back0[0][:], back0[1][:]])
         ra0_sb = sb([P, PASS], F32, "ra0_sb", "back0")
         nc.scalar.copy(ra0_sb[:], ra_ps[0][:])
+
         front1 = sb([P, PASS + HALF], F32, "g_front1", "front")
         back1 = sb([P, HALF], F32, "g_back1", "back1")
         g_turned1 = g_values(1, "b5", front1[:, :PASS], [front1[:, PASS:], back1[:]])
@@ -126,65 +128,67 @@ def tile_list_moment_headpicks_bounded_larger_kernel(tc, xf, ra, gt, rb, cp, old
             for t in range(4):
                 nc.tensor.transpose(x_turned0[a][:, t, :], x0[a][:, t:PASS:4], ident[:])
 
-        shared = sb([P, 2 * PASS], F32, "shared", "g_vals1_1")
-        g_in0, picked = shared[:, :PASS].bitcast(BF16), shared[:, PASS:]
+        shared = sb([P, 2 * PASS], F32, "shared", "g_vals1_0")
+        g_in0, picked1 = shared[:, :PASS].bitcast(BF16), shared[:, PASS:]
         weave(g_in0, g_turned0)
 
         x_turned1 = [bank([P, 2, P], "x_turned1_%d" % a, ("b0", "b7")[a]) for a in range(2)]
-        product = sb([P, PASS], F32, "x_product1", "back1")
-        x_gather(1, product[:], picked)
-        late_in = sb([P, 2 * J + PASS], BF16, "late_in", "back0")
-        x_in0 = late_in[:, J : 2 * J].rearrange("p (a c t) -> p a c t", a=2, t=4)
+        product1 = sb([P, PASS], F32, "x_product1", "back1")
+        x_gather(1, product1[:], picked1)
+        late = sb([P, 2 * J + PASS], BF16, "late", "back0")
+        g_in1, x_in0, x_vals1_1 = late[:, :J], late[:, J : 2 * J], late[:, 2 * J :]
+        x_in0_by_pass = x_in0.rearrange("p (a c t) -> p a c t", a=2, t=4)
+        x_vals1_0 = sb([P, PASS], BF16, "x_vals1_0")
+        nc.gpsimd.tensor_scalar(x_vals1_0[:], product1[:], 1.0, 0.0, ALU.mult, ALU.add)
+        nc.vector.tensor_tensor(x_vals1_1, picked1, ra_ps[1][:], ALU.mult)
+        nc.vector.tensor_tensor(
+            x_in0_by_pass[:, 1, :, :],
+            x_turned0[1][:].rearrange("p t c -> p c t"),
+            ra_back[:].unsqueeze(1).to_broadcast([P, P, 4]),
+            ALU.mult,
+        )
+        for a, x_vals in enumerate((x_vals1_0[:], x_vals1_1)):
+            turn_words(x_vals, x_turned1[a][:])
+        nc.scalar.copy(x_in0_by_pass[:, 0, :, :], x_turned0[0][:].rearrange("p t c -> p c t"))
+        weave(g_in1, g_turned1)
 
-        def weigh_turned(lo, hi):
-            nc.vector.tensor_tensor(
-                x_in0[:, 1, lo:hi, :], x_turned0[1][:, :, lo:hi].rearrange("p t c -> p c t"),
-                ra_back[:].unsqueeze(1).to_broadcast([P, hi - lo, 4]), ALU.mult,
-            )
-
-        rounded = sb([P, PASS], BF16, "x_vals1_0")
-        vals = [rounded[:], late_in[:, 2 * J :]]
-        nc.gpsimd.tensor_scalar(vals[0], product[:], 1.0, 0.0, ALU.mult, ALU.add)
-        weigh_turned(0, P // 2)
-        nc.vector.tensor_tensor(vals[1], picked, ra_ps[1][:], ALU.mult)
-        weigh_turned(P // 2, P)
-        for a in range(2):
-            turn(vals[a], x_turned1[a][:])
-
-        nc.scalar.copy(x_in0[:, 0, :, :], x_turned0[0][:].rearrange("p t c -> p c t"))
-        weave(late_in[:, :J], g_turned1)
-        g_in = [g_in0, late_in[:, :J]]
         g_codes = sb([P, 2, 2 * P], U32, "g_codes", "back1")
         g_scales = sb([P, 2, 2 * P], U8, "g_scales")
-        nc.vector.quantize_mx(g_codes[:, 0, :].bitcast(E5M2), g_scales[:, 0, :], g_in[0])
+        nc.vector.quantize_mx(g_codes[:, 0, :].bitcast(E5M2), g_scales[:, 0, :], g_in0)
         x_codes = [sb([P, 2, P], U32, "x_codes%d" % h) for h in range(2)]
         x_scales = [sb([P, 2, P], U8, "x_scales%d" % h) for h in range(2)]
         nc.vector.quantize_mx(
             x_codes[0][:].rearrange("p a c -> p (a c)").bitcast(E4M3),
             x_scales[0][:].rearrange("p a c -> p (a c)"),
-            late_in[:, J : 2 * J],
+            x_in0,
         )
-        nc.vector.quantize_mx(g_codes[:, 1, :].bitcast(E5M2), g_scales[:, 1, :], g_in[1])
+        nc.vector.quantize_mx(g_codes[:, 1, :].bitcast(E5M2), g_scales[:, 1, :], g_in1)
 
-        def product_pass(acc, h, nh, a, first):
+        def product_pass(acc, h, nh, a):
             span = slice(a * P, (a + 1) * P)
             nc.tensor.matmul_mx(
-                acc, x_codes[h][:, a, :].bitcast(E4M3), x_scales[h][:, a, :],
-                g_codes[:, nh, span].bitcast(E5M2), g_scales[:, nh, span], start=first, stop=not first,
+                acc,
+                x_codes[h][:, a, :].bitcast(E4M3),
+                x_scales[h][:, a, :],
+                g_codes[:, nh, span].bitcast(E5M2),
+                g_scales[:, nh, span],
+                start=(a == 0),
+                stop=(a == 1),
             )
 
         acc0 = bank([P, N], "acc0", "b2")
         for nh in range(2):
             for a in range(2):
-                product_pass(acc0[:, nh * P : (nh + 1) * P], 0, nh, a, a == 0)
+                product_pass(acc0[:, nh * P : (nh + 1) * P], 0, nh, a)
         acc1 = [bank([P, P], "acc1_%d" % nh, ("b3", "b4")[nh]) for nh in range(2)]
         for a in range(2):
-            woven = sb([P, P * 4], BF16, "x_in1_%d" % a)
+            woven = sb([P, PASS], BF16, "x_in1_%d" % a)
             words = woven[:].bitcast(F32).rearrange("p (c u) -> p c u", u=2)
             nc.scalar.copy(words, x_turned1[a][:].rearrange("p u c -> p c u"))
             nc.vector.quantize_mx(x_codes[1][:, a, :].bitcast(E4M3), x_scales[1][:, a, :], woven[:])
             for nh in range(2):
-                product_pass(acc1[nh][:], 1, nh, a, a == 0)
+                product_pass(acc1[nh][:], 1, nh, a)
+
         old_scaled = sb([P, 2, N], F32, "old_scaled", "back0")
         nc.scalar.mul(old_scaled[:], old_sb[:], GAIN)
 

from contextlib import ExitStack

import concourse.mybir as mybir
from concourse.masks import make_identity

K, J, N, T = 256, 1024, 256, 2048
FLOPS = 2 * K * J * N

F32 = mybir.dt.float32
BF16 = mybir.dt.bfloat16
U32 = mybir.dt.uint32
U16 = mybir.dt.uint16
U8 = mybir.dt.uint8
E4M3 = mybir.dt.float8_e4m3fn_x4
E5M2 = mybir.dt.float8_e5m2_x4
ALU = mybir.AluOpType
COPY = mybir.ActivationFunctionType.Copy

P = 128
PASS = 512
HALF = PASS // 2
GROUP = 16
GAIN = 0.04
RA_ROW, CP_ROW, RB_ROW, SPARE_ROW = 24, 54, 56, 64


def tile_list_moment_headpicks_bounded_larger_kernel(tc, xf, ra, gt, rb, cp, old, offs, offs2, out):
    nc = tc.nc
    with ExitStack() as ctx:
        keep = ctx.enter_context(tc.tile_pool(name="keep", bufs=1))
        psum = ctx.enter_context(tc.psum_pool(name="psum", bufs=1))

        def sb(shape, dtype, name, tag=None):
            return keep.tile(shape, dtype, name=name, tag=tag or name, align_bytes=64)

        def bank(shape, name, tag):
            return psum.tile(shape, F32, name=name, tag=tag)

        x_list = keep.tile([P, J // GROUP], U16, name="x_list")
        g_list = keep.tile([P, J // GROUP], U16, name="g_list")
        g_win = [sb([P, T], F32, "g_win%d" % h) for h in range(2)]
        x_win = [sb([P, T], F32, "x_win%d" % h) for h in range(2)]
        old_sb = sb([P, 2, N], F32, "old_sb")
        rows = sb([P, P], F32, "rows", "front")
        ra_back = sb([P, 4], F32, "ra_back")
        nc.scalar.dma_start(rows[RB_ROW : RB_ROW + 8, :], rb.rearrange("o (m p) -> (o m) p", p=P))
        nc.scalar.dma_start(rows[CP_ROW : CP_ROW + 2, :], cp.rearrange("(m p) o -> m (p o)", p=P))
        nc.sync.dma_start(rows[RA_ROW : RA_ROW + 8, :], ra.rearrange("o (m p) -> (o m) p", p=P))
        nc.sync.dma_start(g_list[:], offs2)
        nc.sync.dma_start(g_win[0][:], gt[0:P, :])
        nc.sync.dma_start(g_win[1][:], gt[P : 2 * P, :])
        nc.sync.dma_start(x_list[:], offs)
        nc.sync.dma_start(x_win[0][:], xf[0:P, :])
        nc.sync.dma_start(x_win[1][:], xf[P : 2 * P, :])
        nc.sync.dma_start(ra_back[:], ra[:, PASS:].rearrange("o (p t) -> (o p) t", t=4))
        nc.sync.dma_start(old_sb[:], old.rearrange("(h p) n -> p h n", p=P))

        nc.vector.memset(rows[0:RA_ROW, :], 0.0)
        nc.vector.memset(rows[32:CP_ROW, :], 0.0)
        zero = sb([P, 1], F32, "zero")
        nc.vector.memset(zero[SPARE_ROW:P, :], 0.0)
        nc.scalar.activation(rows[SPARE_ROW:P, :], zero[SPARE_ROW:P, :].to_broadcast([P - SPARE_ROW, P]), COPY)
        ident = sb([P, P], F32, "ident")
        make_identity(nc, ident[:])

        cols_ps = bank([P, P], "cols_ps", "b0")
        nc.tensor.transpose(cols_ps[:], rows[:], ident[:])
        cols = sb([P, SPARE_ROW - RA_ROW], F32, "cols")
        nc.vector.tensor_copy(cols[:], cols_ps[:, RA_ROW:SPARE_ROW])

        def spread(first_col, name, tag):
            wide = bank([P, PASS], name, tag)
            for m in range(PASS // P):
                col = cols[:, first_col + m : first_col + m + 1]
                nc.tensor.transpose(wide[:, m * P : (m + 1) * P], col.to_broadcast([P, P]), ident[:])
            return wide

        rb_ps = {a: spread(RB_ROW - RA_ROW + 4 * a, "rb_ps%d" % a, "b%d" % (2 + a)) for a in (1, 0)}
        ra_ps = [spread(4 * a, "ra_ps%d" % a, ("b1", "b4")[a]) for a in range(2)]

        def listed(window, offsets, lo, hi):
            return window[:].indirect(offsets[:, lo // GROUP : hi // GROUP])

        def turn_words(vals, dst):
            for u in range(2):
                nc.tensor.transpose(dst[:, u, :], vals.bitcast(F32)[:, u : 2 * P : 2], ident[:])

        def g_values(h, tag, front, back):
            nc.vector.tensor_copy(front, listed(g_win[h], g_list, 0, PASS))
            for b in range(2):
                lo = PASS + b * HALF
                nc.scalar.activation(back[b], listed(g_win[h], g_list, lo, lo + HALF), COPY)
            vals = [sb([P, PASS], BF16, "g_vals%d_%d" % (h, a)) for a in range(2)]
            bound = cols[:, CP_ROW - RA_ROW + h : CP_ROW - RA_ROW + h + 1]
            for dst, src, weight in (
                (vals[1][:, :HALF], back[0], rb_ps[1][:, :HALF]),
                (vals[0][:], front, rb_ps[0][:]),
                (vals[1][:, HALF:], back[1], rb_ps[1][:, HALF:]),
            ):
                nc.vector.scalar_tensor_tensor(dst, src, bound, weight, ALU.min, ALU.mult)
            turned = bank([P, 2, 2, P], "g_turned%d" % h, tag)
            for a in range(2):
                turn_words(vals[a][:], turned[:, a, :, :])
            return turned

        def x_gather(h, product, picked):
            nc.vector.tensor_tensor(product, listed(x_win[h], x_list, 0, PASS), ra0_sb[:], ALU.mult)
            nc.scalar.activation(picked, listed(x_win[h], x_list, PASS, J), COPY)

        def weave(woven, turned):
            words = woven.bitcast(F32).rearrange("p (a c u) -> p a c u", a=2, u=2)
            nc.scalar.copy(words, turned[:].rearrange("p a u c -> p a c u"))

        front0 = sb([P, PASS], F32, "g_front0", "front")
        back0 = [sb([P, HALF], F32, "g_back0_%d" % b, "back%d" % b) for b in range(2)]
        g_turned0 = g_values(0, "b0", front0[:], [back0[0][:], back0[1][:]])
        ra0_sb = sb([P, PASS], F32, "ra0_sb", "back0")
        nc.scalar.copy(ra0_sb[:], ra_ps[0][:])

        front1 = sb([P, PASS + HALF], F32, "g_front1", "front")
        back1 = sb([P, HALF], F32, "g_back1", "back1")
        g_turned1 = g_values(1, "b5", front1[:, :PASS], [front1[:, PASS:], back1[:]])

        x_turned0 = [bank([P, 4, P], "x_turned0_%d" % a, ("b1", "b6")[a]) for a in range(2)]
        x0 = [sb([P, PASS], F32, "x_product0", "front"), sb([P, PASS], F32, "x_picked0", "g_vals0_1")]
        x_gather(0, x0[0][:], x0[1][:])
        for a in (1, 0):
            for t in range(4):
                nc.tensor.transpose(x_turned0[a][:, t, :], x0[a][:, t:PASS:4], ident[:])

        shared = sb([P, 2 * PASS], F32, "shared", "g_vals1_0")
        g_in0, picked1 = shared[:, :PASS].bitcast(BF16), shared[:, PASS:]
        weave(g_in0, g_turned0)

        x_turned1 = [bank([P, 2, P], "x_turned1_%d" % a, ("b0", "b7")[a]) for a in range(2)]
        product1 = sb([P, PASS], F32, "x_product1", "back1")
        x_gather(1, product1[:], picked1)
        late = sb([P, 2 * J + PASS], BF16, "late", "back0")
        g_in1, x_in0, x_vals1_1 = late[:, :J], late[:, J : 2 * J], late[:, 2 * J :]
        x_in0_by_pass = x_in0.rearrange("p (a c t) -> p a c t", a=2, t=4)
        x_vals1_0 = sb([P, PASS], BF16, "x_vals1_0")
        nc.gpsimd.tensor_scalar(x_vals1_0[:], product1[:], 1.0, 0.0, ALU.mult, ALU.add)
        nc.vector.tensor_tensor(x_vals1_1, picked1, ra_ps[1][:], ALU.mult)
        nc.vector.tensor_tensor(
            x_in0_by_pass[:, 1, :, :],
            x_turned0[1][:].rearrange("p t c -> p c t"),
            ra_back[:].unsqueeze(1).to_broadcast([P, P, 4]),
            ALU.mult,
        )
        for a, x_vals in enumerate((x_vals1_0[:], x_vals1_1)):
            turn_words(x_vals, x_turned1[a][:])
        nc.scalar.copy(x_in0_by_pass[:, 0, :, :], x_turned0[0][:].rearrange("p t c -> p c t"))
        weave(g_in1, g_turned1)

        g_codes = sb([P, 2, 2 * P], U32, "g_codes", "back1")
        g_scales = sb([P, 2, 2 * P], U8, "g_scales")
        nc.vector.quantize_mx(g_codes[:, 0, :].bitcast(E5M2), g_scales[:, 0, :], g_in0)
        x_codes = [sb([P, 2, P], U32, "x_codes%d" % h) for h in range(2)]
        x_scales = [sb([P, 2, P], U8, "x_scales%d" % h) for h in range(2)]
        nc.vector.quantize_mx(
            x_codes[0][:].rearrange("p a c -> p (a c)").bitcast(E4M3),
            x_scales[0][:].rearrange("p a c -> p (a c)"),
            x_in0,
        )
        nc.vector.quantize_mx(g_codes[:, 1, :].bitcast(E5M2), g_scales[:, 1, :], g_in1)

        def product_pass(acc, h, nh, a):
            span = slice(a * P, (a + 1) * P)
            nc.tensor.matmul_mx(
                acc,
                x_codes[h][:, a, :].bitcast(E4M3),
                x_scales[h][:, a, :],
                g_codes[:, nh, span].bitcast(E5M2),
                g_scales[:, nh, span],
                start=(a == 0),
                stop=(a == 1),
            )

        acc0 = bank([P, N], "acc0", "b2")
        for nh in range(2):
            for a in range(2):
                product_pass(acc0[:, nh * P : (nh + 1) * P], 0, nh, a)
        acc1 = [bank([P, P], "acc1_%d" % nh, ("b3", "b4")[nh]) for nh in range(2)]
        for a in range(2):
            woven = sb([P, PASS], BF16, "x_in1_%d" % a)
            words = woven[:].bitcast(F32).rearrange("p (c u) -> p c u", u=2)
            nc.scalar.copy(words, x_turned1[a][:].rearrange("p u c -> p c u"))
            nc.vector.quantize_mx(x_codes[1][:, a, :].bitcast(E4M3), x_scales[1][:, a, :], woven[:])
            for nh in range(2):
                product_pass(acc1[nh][:], 1, nh, a)

        old_scaled = sb([P, 2, N], F32, "old_scaled", "back0")
        nc.scalar.mul(old_scaled[:], old_sb[:], GAIN)

        def finish(acc, h, lo, hi, queue):
            result = sb([P, hi - lo], F32, "result%d_%d" % (h, lo))
            nc.vector.scalar_tensor_tensor(result[:], acc, GAIN, old_scaled[:, h, lo:hi], ALU.mult, ALU.max)
            queue.dma_start(out[h * P : (h + 1) * P, lo:hi], result[:])

        finish(acc0[:], 0, 0, N, nc.sync)
        finish(acc1[0][:], 1, 0, P, nc.scalar)
        finish(acc1[1][:], 1, P, N, nc.sync)
